import numpy as np
import ml_dtypes


def mxq(x, axis, fmt="e4m3"):
    dtype, down = {"e4m3": (ml_dtypes.float8_e4m3fn, 7), "e5m2": (ml_dtypes.float8_e5m2, 14)}[fmt]
    v = np.moveaxis(np.asarray(x, np.float32).astype(ml_dtypes.bfloat16).astype(np.float64), axis, -1)
    blocks = v.reshape(v.shape[:-1] + (-1, 32))
    amax = np.abs(blocks).max(-1, keepdims=True)
    byte = np.maximum(np.where(amax > 0, np.frexp(amax)[1] - 1 + 127, 0) - down, 1)
    scale = np.exp2(byte - 127.0)
    codes = (blocks / scale).astype(np.float32).astype(dtype).astype(np.float64)
    return np.moveaxis((codes * scale).reshape(v.shape), -1, axis)


WIDE = False


def mx_kscale(k):
    if not WIDE:
        return np.ones(k)
    levels = np.array([10, -10, 5, -5, 0])
    if k % 512:
        return np.exp2(np.random.permutation(np.resize(levels, k // 32))).repeat(32)
    a = np.empty((k // 512, 16))
    for p in range(k // 512):
        a[p, :8] = np.random.permutation(np.resize(levels, 8))
        for g in range(8):
            far = levels[np.abs(levels - a[p, g]) >= 10]
            a[p, g + 8] = far[np.random.randint(len(far))]
    return np.exp2(a.ravel()).repeat(32)


def f64(x):
    return np.asarray(x).astype(np.float64)


def striped(idx):
    return np.tile(idx.reshape(-1, 16).T, (8, 1)).astype(np.uint16)


def unstriped(offs):
    return offs[:16].T.reshape(-1).astype(np.int64)


E2M1 = np.array([0.0, 0.5, 1.0, 1.5, 2.0, 3.0, 4.0, 6.0, -0.0, -0.5, -1.0, -1.5, -2.0, -3.0, -4.0, -6.0])


def pack_weight(w, fmt):
    k, n = w.shape
    w = f64(np.asarray(w, np.float32).astype(ml_dtypes.bfloat16)).reshape(k // 32, 32, n)
    amax = np.abs(w).max(1)
    if fmt == "e4m3":
        byte = np.frexp(amax)[1] - 1 + 127 - 7
    else:
        mant, ex = np.frexp(amax / 6.0)
        byte = np.where(mant > 0.5, ex, ex - 1) + 127
    byte = np.clip(np.where(amax > 0, byte, 1), 1, 254)
    scaled = (w * np.exp2(127.0 - byte)[:, None, :]).reshape(k, n).astype(np.float32)
    by_word = np.ascontiguousarray(scaled.reshape(k // 512, 128, 4, n).transpose(0, 1, 3, 2))
    if fmt == "e4m3":
        words = by_word.astype(ml_dtypes.float8_e4m3fn).view(np.uint8)
    else:
        c = by_word.astype(ml_dtypes.float4_e2m1fn).view(np.uint8) & 0xF
        words = (c[..., 0::2] | (c[..., 1::2] << 4)).reshape(k // 512, 128, 2 * n)
    return np.ascontiguousarray(words), np.ascontiguousarray(byte.astype(np.uint8).reshape(k // 512, 16, n))


def unpack_weight(words, scales, fmt):
    g, _, n = scales.shape
    words = np.ascontiguousarray(words).reshape(g, 128, n, -1)
    if fmt == "e4m3":
        vals = words.view(ml_dtypes.float8_e4m3fn).astype(np.float64)
    else:
        nib = np.empty((g, 128, n, 4), np.uint8)
        nib[..., 0::2] = words & 0xF
        nib[..., 1::2] = words >> 4
        vals = E2M1[nib]
    vals = vals * np.repeat(np.exp2(scales.astype(np.float64) - 127.0), 8, axis=1)[..., None]
    return vals.transpose(0, 1, 3, 2).reshape(g * 512, n)


def gelu(v):
    return 0.5 * v * (1.0 + np.tanh(np.sqrt(2.0 / np.pi) * (v + 0.044715 * v**3)))


K, H, N, T, S, T2 = 1024, 512, 768, 4096, 1024, 2048


def setup_inputs():
    n = np.random.standard_normal
    s = mx_kscale(K)[:, None]
    u = mx_kscale(H)[:, None]
    tab_words, tab_scales = pack_weight(n((K, T)) * s, "e4m3")
    wa_words, wa_scales = pack_weight(n((K, H)) / np.sqrt(K) / s * u.T, "e2m1")
    return {
        "tab_words": tab_words,
        "tab_scales": tab_scales,
        "offs": striped(np.random.permutation(T)[:S]),
        "offs2": striped(np.random.permutation(T)[:S]),
        "offs3": striped(np.random.permutation(T2)[:S]),
        "wa_words": wa_words,
        "wa_scales": wa_scales,
        "ga": np.random.uniform(0.5, 2.0, H).astype(np.float32),
        "wb": (1.2 * n((K, H)) / np.sqrt(K) / s * u.T).astype(np.float32),
        "wc": (1.2 * n((H, N)) / np.sqrt(H) / u).astype(np.float32),
        "interf": (0.8 * n((N, S))).astype(np.float32),
        "gr": np.exp(0.4 * n(N)).astype(np.float32),
        "wgo": np.exp(0.3 * n((128, S))).astype(np.float32),
    }


def reference(tab_words, tab_scales, offs, offs2, offs3, wa_words, wa_scales, ga, wb, wc, interf, gr, wgo):
    TW = unpack_weight(tab_words, tab_scales, "e4m3")
    v = TW[:, unstriped(offs)]
    v2 = TW[:, unstriped(offs2)]
    up = unpack_weight(wa_words, wa_scales, "e2m1").T @ v
    gw = mxq(f64(wb), 0, "e4m3").T @ v2
    z = np.maximum(f64(ga)[:, None] * up, gw)
    q = mxq(f64(wc), 0, "e4m3").T @ mxq(z, 0, "e4m3")
    y = f64(gr)[:, None] * np.tanh(q + f64(interf))
    out = np.zeros((N, T2))
    out[:, unstriped(offs3)] = np.tile(f64(wgo), (N // 128, 1)) * y
    return out

@@ -1,0 +1,320 @@
+from contextlib import ExitStack
+
+import concourse.mybir as mybir
+from concourse.masks import make_identity
+
+K, H, N, T, S, T2 = 1024, 512, 768, 4096, 1024, 2048
+FLOPS = 2 * (2 * K * H * S + H * N * S)
+
+F32 = mybir.dt.float32
+BF16 = mybir.dt.bfloat16
+I32 = mybir.dt.int32
+U32 = mybir.dt.uint32
+U16 = mybir.dt.uint16
+U8 = mybir.dt.uint8
+E4M3 = mybir.dt.float8_e4m3fn_x4
+E2M1 = mybir.dt.float4_e2m1fn_x4
+MULT = mybir.AluOpType.mult
+ADD = mybir.AluOpType.add
+MAX = mybir.AluOpType.max
+COPY = mybir.ActivationFunctionType.Copy
+TANH = mybir.ActivationFunctionType.Tanh
+
+P = 128
+PACK = 4
+PASSES = K // (P * PACK)
+HALF = 512
+HALVES = S // HALF
+CHUNKS = HALF // P
+ROW_TILES = N // P
+WC_COLS = 256
+PAGES = 3
+SPLIT_TILES = 2
+SHIFT_ROWS = 112
+BANKS = {"up": 2, "gw": 3, "q": 1, "sum": 1, "back": 1}
+
+
+def tile_list_gateway_rate_scores_kernel(
+    tc, tab_words, tab_scales, offs, offs2, offs3, wa_words, wa_scales, ga, wb, wc, interf, gr, wgo, out
+):
+    nc = tc.nc
+    with ExitStack() as ctx:
+        keep = ctx.enter_context(tc.tile_pool(name="keep", bufs=1))
+        ring = ctx.enter_context(tc.tile_pool(name="ring", bufs=3))
+        psum = ctx.enter_context(tc.psum_pool(name="psum", bufs=2))
+
+        def held(shape, dtype, name, tag=None):
+            return keep.tile(shape, dtype, name=name, tag=tag or name, align_bytes=64)
+
+        def bank(name, tag):
+            return psum.tile([P, HALF], F32, name=name, tag=tag, bufs=BANKS[tag])
+
+        tab_sc = held([P, T], U8, "tab_sc")
+        nc.vector.memset(tab_sc[:].bitcast(I32), 0)
+        pages = [held([P, T2], F32, "page%d" % g) for g in range(PAGES)]
+        for page in pages:
+            nc.vector.memset(page[:], 0.0)
+
+        gains_rows = held([P, P], F32, "gains_rows")
+        nc.gpsimd.memset(gains_rows[:], 0.0)
+        wa_sc_raw = held([P, PASSES * H], U8, "wa_sc_raw")
+        nc.gpsimd.memset(wa_sc_raw[:].bitcast(I32), 0)
+        up_sc_shifted = held([P, S], U8, "up_sc_shifted")
+        nc.gpsimd.memset(up_sc_shifted[:].bitcast(I32), 0)
+        ident = held([P, P], F32, "ident")
+        make_identity(nc, ident[:])
+        nc.gpsimd.dma_start(
+            gains_rows[0:PACK, :].rearrange("t (b e) -> t b e", e=8),
+            ga.rearrange("(b t e) -> t b e", t=PACK, e=8),
+        )
+        nc.gpsimd.dma_start(gains_rows[PACK : PACK + ROW_TILES, :], gr.rearrange("(i p) -> i p", p=P))
+        for q in range(4):
+            nc.gpsimd.dma_start(
+                wa_sc_raw[32 * q : 32 * q + 4, :].bitcast(I32).rearrange("r (a w) -> r a w", a=PASSES),
+                wa_scales[:, 4 * q : 4 * q + 4, :].bitcast(I32).rearrange("a r w -> r a w"),
+            )
+
+        def load_list(name, src):
+            tile = keep.tile([P, S // 16], U16, name=name)
+            nc.sync.dma_start(tile[:], src)
+            return tile
+
+        list_up = load_list("list_up", offs)
+        list_gw = load_list("list_gw", offs2)
+        list_out = load_list("list_out", offs3)
+        tab = [held([P, T], U32, "tab%d" % a) for a in range(PASSES)]
+        wb_raw = [held([P, PACK, H], F32, "wb_raw%d" % a) for a in range(PASSES)]
+        wa_raw = held([P, PASSES * 2 * H], U8, "wa_raw")
+
+        def load_table(a, pieces):
+            words = tab_words[a].rearrange("p t i -> p (t i)").bitcast(I32)
+            for u in range(pieces):
+                cols = slice(u * T // pieces, (u + 1) * T // pieces)
+                nc.sync.dma_start(tab[a][:].bitcast(I32)[:, cols], words[:, cols])
+
+        load_table(0, 4)
+        nc.sync.dma_start(
+            wa_raw[:].bitcast(I32).rearrange("p (a w) -> p a w", a=PASSES),
+            wa_words.bitcast(I32).rearrange("a p w -> p a w"),
+        )
+        for q in range(4):
+            nc.sync.dma_start(
+                tab_sc[32 * q : 32 * q + 4 * PASSES, :].bitcast(I32),
+                tab_scales[:, 4 * q : 4 * q + 4, :].bitcast(I32),
+            )
+        for a in range(PASSES):
+            nc.sync.dma_start(
+                wb_raw[a][:], wb[512 * a : 512 * (a + 1), :].rearrange("(p j) c -> p j c", j=PACK)
+            )
+        load_table(1, 1)
+
+        gains_bank = bank("gains_bank", "back")
+        nc.tensor.transpose(gains_bank[:, 0:P], gains_rows[:], ident[:])
+        gains = held([P, 16], F32, "gains")
+        nc.scalar.copy(gains[:], gains_bank[:, 0:16])
+
+        wa_codes = held([P, PASSES * 2 * H], U8, "wa_codes")
+        wa_sc = held([P, PASSES * H], U8, "wa_sc")
+        for dst, src in ((wa_codes, wa_raw), (wa_sc, wa_sc_raw)):
+            for a in range(PASSES):
+                nc.gpsimd.tensor_copy(
+                    dst[:].bitcast(I32).rearrange("p (a t b e) -> p a t b e", a=PASSES, t=PACK, b=16)[:, a],
+                    src[:].bitcast(I32).rearrange("p (a b t e) -> p a t b e", a=PASSES, t=PACK, b=16)[:, a],
+                )
+
+        up_sc = held([P, S], U8, "up_sc")
+        gw_sc = held([P, S], U8, "gw_sc")
+        nc.vector.tensor_copy(up_sc[:], tab_sc[:].indirect(list_up[:]))
+        nc.vector.tensor_copy(gw_sc[:], tab_sc[:].indirect(list_gw[:]))
+        nc.sync.dma_start(
+            up_sc_shifted[0:SHIFT_ROWS, :].bitcast(I32), up_sc[4 : 4 + SHIFT_ROWS, :].bitcast(I32)
+        )
+        up0 = held([P, S], U32, "up0")
+        gw0 = held([P, S], U32, "gw0")
+        nc.vector.tensor_copy(up0[:], tab[0][:].indirect(list_up[:]))
+        nc.vector.tensor_copy(gw0[:], tab[0][:].indirect(list_gw[:]))
+
+        wb_codes, wb_sc = {}, {}
+
+        def quantise_wb(a, pair, copy):
+            rounded = held([P, 2 * P * PACK], BF16, "wb_bf%d_%d" % (a, pair))
+            for u in range(2):
+                copy(
+                    rounded[:].rearrange("p (u b h i j) -> p u b h j i", u=2, b=16, h=2, i=4)[:, u],
+                    wb_raw[a][:].rearrange("p j (b t h i) -> p t b h j i", t=PACK, h=2, i=4)[:, 2 * pair + u],
+                )
+            codes = held([P, 2 * P], U32, "wb_codes%d_%d" % (a, pair))
+            scales = held([P, 2 * P], U8, "wb_sc%d_%d" % (a, pair))
+            nc.vector.quantize_mx(codes[:].bitcast(E4M3), scales[:], rounded[:])
+            wb_codes[a, pair] = codes
+            wb_sc[a, pair] = scales
+
+        for a in range(PASSES):
+            for pair in range(2):
+                quantise_wb(a, pair, nc.scalar.copy)
+
+        up1, gw1 = [], []
+        for h in range(HALVES):
+            cut = slice(h * HALF // 16, (h + 1) * HALF // 16)
+            for name, picked, order in (("up1_%d", up1, list_up), ("gw1_%d", gw1, list_gw)):
+                tile = held([P, HALF], U32, name % h)
+                nc.vector.tensor_copy(tile[:], tab[1][:].indirect(order[:, cut]))
+                picked.append(tile)
+
+        wc_raw = held([P, PACK, N], F32, "wc_raw", tag="wb_raw0")
+        wc_by_slot = wc.rearrange("(b t e) n -> t b e n", t=PACK, e=8)
+        for t in range(PACK):
+            nc.sync.dma_start(wc_raw[:, t, :], wc_by_slot[t])
+        first = held([P, 2, S], F32, "first", tag="wb_raw1")
+        rest = held([P, ROW_TILES - 1, S], F32, "rest", tag="tab0")
+        wgo_sb = first[:, 1, :]
+        interf_sb = [first[:, 0, :]] + [rest[:, i, :] for i in range(ROW_TILES - 1)]
+        for i in range(ROW_TILES):
+            nc.sync.dma_start(interf_sb[i], interf[P * i : P * (i + 1), :])
+            if i == 0:
+                nc.sync.dma_start(wgo_sb, wgo)
+
+        def up_pass(acc, h, t, a):
+            cols = slice(h * HALF, (h + 1) * HALF)
+            nc.tensor.matmul_mx(
+                acc[:],
+                lhsT=wa_codes[:, 2 * (a * H + t * P) : 2 * (a * H + (t + 1) * P)].bitcast(E2M1),
+                lhsT_scale=wa_sc[:, a * H + t * P : a * H + (t + 1) * P],
+                rhs=(up0[:, cols] if a == 0 else up1[h][:]).bitcast(E4M3),
+                rhs_scale=(up_sc if a == 0 else up_sc_shifted)[:, cols],
+                start=(a == 0),
+                stop=(a == PASSES - 1),
+            )
+
+        def gw_pass(acc, h, c, t, a):
+            j0 = h * HALF + c * P
+            nc.tensor.matmul_mx(
+                acc[:, t * P : (t + 1) * P],
+                lhsT=wb_codes[a, t // 2][:, t % 2 * P : (t % 2 + 1) * P].bitcast(E4M3),
+                lhsT_scale=wb_sc[a, t // 2][:, t % 2 * P : (t % 2 + 1) * P],
+                rhs=(gw0[:, j0 : j0 + P] if a == 0 else gw1[h][:, c * P : (c + 1) * P]).bitcast(E4M3),
+                rhs_scale=gw_sc[4 * a : P, j0 : j0 + P],
+                start=(a == 0 and t == 0),
+                stop=(a == PASSES - 1 and t == PACK - 1),
+            )
+
+        z_codes, z_sc = [], []
+
+        def first_stage(h):
+            scaled = held([P, PACK, HALF], F32, "scaled%d" % h)
+            z_bf = held([P, HALF * PACK], BF16, "z_bf%d" % h)
+            for t in range(PACK):
+                up_bank = bank("up%d_%d" % (h, t), "up")
+                for a in range(PASSES):
+                    up_pass(up_bank, h, t, a)
+                nc.scalar.activation(scaled[:, t, :], up_bank[:], COPY, scale=gains[:, t : t + 1])
+            if h == 0:
+                quantise_wc(0)
+            for c in range(CHUNKS):
+                gw_bank = bank("gw%d_%d" % (h, c), "gw")
+                for a in range(PASSES):
+                    for t in range(PACK):
+                        gw_pass(gw_bank, h, c, t, a)
+                nc.vector.tensor_tensor(
+                    z_bf[:, c * HALF : (c + 1) * HALF].rearrange("p (g i t) -> p g t i", i=4, t=PACK),
+                    gw_bank[:].rearrange("p (t g i) -> p g t i", t=PACK, i=4),
+                    scaled[:, :, c * P : (c + 1) * P].rearrange("p t (g i) -> p g t i", i=4),
+                    MAX,
+                )
+            codes = held([P, HALF], U32, "z_codes%d" % h)
+            scales = held([P, HALF], U8, "z_sc%d" % h)
+            nc.vector.quantize_mx(codes[:].bitcast(E4M3), scales[:], z_bf[:])
+            z_codes.append(codes)
+            z_sc.append(scales)
+
+        wc_codes, wc_sc = [], []
+
+        def quantise_wc(u):
+            rounded = held([P, WC_COLS * PACK], BF16, "wc_bf%d" % u)
+            nc.scalar.copy(
+                rounded[:].rearrange("p (g i t) -> p g t i", i=4, t=PACK),
+                wc_raw[:, :, u * WC_COLS : (u + 1) * WC_COLS].rearrange("p t (g i) -> p g t i", i=4),
+            )
+            codes = held([P, WC_COLS], U32, "wc_codes%d" % u)
+            scales = held([P, WC_COLS], U8, "wc_sc%d" % u)
+            nc.vector.quantize_mx(codes[:].bitcast(E4M3), scales[:], rounded[:])
+            wc_codes.append(codes)
+            wc_sc.append(scales)
+
+        q_sb, turned, y_sb = {}, {}, {}
+
+        def product(i, h):
+            u, c0 = divmod(i * P, WC_COLS)
+            q_bank = bank("q%d_%d" % (i, h), "q")
+            nc.tensor.matmul_mx(
+                q_bank[:],
+                lhsT=wc_codes[u][:, c0 : c0 + P].bitcast(E4M3),
+                lhsT_scale=wc_sc[u][:, c0 : c0 + P],
+                rhs=z_codes[h][:].bitcast(E4M3),
+                rhs_scale=z_sc[h][:],
+                start=True,
+                stop=True,
+            )
+            q_sb[i, h] = ring.tile([P, HALF], F32, name="q_sb")
+            if (i, h) == (0, 0):
+                nc.vector.tensor_tensor(q_sb[i, h][:], q_bank[:], interf_sb[i][:, 0:HALF], ADD)
+                turned[i, h] = ring.tile([P, HALF], F32, name="turned")
+                nc.scalar.activation(turned[i, h][:], q_sb[i, h][:], TANH)
+                place(i, h, turned[i, h])
+            else:
+                nc.scalar.copy(q_sb[i, h][:], q_bank[:])
+
+        def shift_and_tanh(i, h):
+            sum_bank = bank("sum%d_%d" % (i, h), "sum")
+            for c in range(CHUNKS):
+                cols = slice(c * P, (c + 1) * P)
+                j0 = h * HALF + c * P
+                nc.tensor.matmul(
+                    sum_bank[:, cols], q_sb[i, h][:, cols], ident[:], start=True, stop=False, is_transpose=True
+                )
+                nc.tensor.matmul(
+                    sum_bank[:, cols], interf_sb[i][:, j0 : j0 + P], ident[:], start=False, stop=True, is_transpose=True
+                )
+            turned[i, h] = ring.tile([P, HALF], F32, name="turned")
+            nc.scalar.activation(turned[i, h][:], sum_bank[:], TANH)
+
+        def turn_back(i, h):
+            back_bank = bank("back%d_%d" % (i, h), "back")
+            for c in range(CHUNKS):
+                cols = slice(c * P, (c + 1) * P)
+                nc.tensor.transpose(back_bank[:, cols], turned[i, h][:, cols], ident[:])
+            place(i, h, back_bank)
+
+        def place(i, h, rates):
+            half = slice(h * HALF, (h + 1) * HALF)
+            page = pages[i % PAGES]
+            gain = gains[:, PACK + i : PACK + i + 1]
+            if i < SPLIT_TILES:
+                y_half = held([P, HALF], F32, "y_half%d_%d" % (i, h))
+                nc.scalar.activation(y_half[:], rates[:], COPY, scale=gain)
+                nc.vector.tensor_tensor(
+                    page[:].indirect(list_out[:, h * HALF // 16 : (h + 1) * HALF // 16]), y_half[:], wgo_sb[:, half], MULT
+                )
+            else:
+                if h == 0:
+                    y_sb[i] = ring.tile([P, S], F32, name="y")
+                nc.scalar.activation(y_sb[i][:, half], rates[:], COPY, scale=gain)
+                if h == HALVES - 1:
+                    nc.vector.tensor_tensor(page[:].indirect(list_out[:]), y_sb[i][:], wgo_sb, MULT)
+            if h == HALVES - 1:
+                nc.sync.dma_start(out[P * i : P * (i + 1), :], page[:])
+
+        units = [(i, h) for h in range(HALVES) for i in range(SPLIT_TILES)]
+        units = units + [(i, h) for i in range(SPLIT_TILES, ROW_TILES) for h in range(HALVES)]
+        first_stage(0)
+        product(*units[0])
+        first_stage(1)
+        for step in range(1, len(units) + 2):
+            if step < len(units):
+                product(*units[step])
+            if 2 <= step <= len(units):
+                shift_and_tanh(*units[step - 1])
+            if step >= 3:
+                turn_back(*units[step - 2])
+            if step in (2, 3):
+                quantise_wc(step - 1)

@@ -29,9 +29,9 @@ CHUNKS = HALF // P
 ROW_TILES = N // P
 WC_COLS = 256
 PAGES = 3
-SPLIT_TILES = 2
+SPLIT_TILES = 3
 SHIFT_ROWS = 112
-BANKS = {"up": 2, "gw": 3, "q": 1, "sum": 1, "back": 1}
+BANKS = {"up": 2, "gw": 3, "back": 3}
 
 
 def tile_list_gateway_rate_scores_kernel(
@@ -40,7 +40,7 @@ def tile_list_gateway_rate_scores_kernel(
     nc = tc.nc
     with ExitStack() as ctx:
         keep = ctx.enter_context(tc.tile_pool(name="keep", bufs=1))
-        ring = ctx.enter_context(tc.tile_pool(name="ring", bufs=3))
+        ring = ctx.enter_context(tc.tile_pool(name="ring", bufs=4))
         psum = ctx.enter_context(tc.psum_pool(name="psum", bufs=2))
 
         def held(shape, dtype, name, tag=None):
@@ -63,16 +63,6 @@ def tile_list_gateway_rate_scores_kernel(
         nc.gpsimd.memset(up_sc_shifted[:].bitcast(I32), 0)
         ident = held([P, P], F32, "ident")
         make_identity(nc, ident[:])
-        nc.gpsimd.dma_start(
-            gains_rows[0:PACK, :].rearrange("t (b e) -> t b e", e=8),
-            ga.rearrange("(b t e) -> t b e", t=PACK, e=8),
-        )
-        nc.gpsimd.dma_start(gains_rows[PACK : PACK + ROW_TILES, :], gr.rearrange("(i p) -> i p", p=P))
-        for q in range(4):
-            nc.gpsimd.dma_start(
-                wa_sc_raw[32 * q : 32 * q + 4, :].bitcast(I32).rearrange("r (a w) -> r a w", a=PASSES),
-                wa_scales[:, 4 * q : 4 * q + 4, :].bitcast(I32).rearrange("a r w -> r a w"),
-            )
 
         def load_list(name, src):
             tile = keep.tile([P, S // 16], U16, name=name)
@@ -97,15 +87,26 @@ def tile_list_gateway_rate_scores_kernel(
             wa_raw[:].bitcast(I32).rearrange("p (a w) -> p a w", a=PASSES),
             wa_words.bitcast(I32).rearrange("a p w -> p a w"),
         )
-        for q in range(4):
-            nc.sync.dma_start(
-                tab_sc[32 * q : 32 * q + 4 * PASSES, :].bitcast(I32),
-                tab_scales[:, 4 * q : 4 * q + 4, :].bitcast(I32),
-            )
+        for a in range(PASSES):
+            for q in range(4):
+                nc.sync.dma_start(
+                    tab_sc[32 * q + 4 * a : 32 * q + 4 * a + 4, :].bitcast(I32),
+                    tab_scales[a, 4 * q : 4 * q + 4, :].bitcast(I32),
+                )
         for a in range(PASSES):
             nc.sync.dma_start(
                 wb_raw[a][:], wb[512 * a : 512 * (a + 1), :].rearrange("(p j) c -> p j c", j=PACK)
             )
+        for q in range(4):
+            nc.sync.dma_start(
+                wa_sc_raw[32 * q : 32 * q + 4, :].bitcast(I32).rearrange("r (a w) -> r a w", a=PASSES),
+                wa_scales[:, 4 * q : 4 * q + 4, :].bitcast(I32).rearrange("a r w -> r a w"),
+            )
+        nc.sync.dma_start(
+            gains_rows[0:PACK, :].rearrange("t (b e) -> t b e", e=8),
+            ga.rearrange("(b t e) -> t b e", t=PACK, e=8),
+        )
+        nc.sync.dma_start(gains_rows[PACK : PACK + ROW_TILES, :], gr.rearrange("(i p) -> i p", p=P))
         load_table(1, 1)
 
         gains_bank = bank("gains_bank", "back")
@@ -116,11 +117,10 @@ def tile_list_gateway_rate_scores_kernel(
         wa_codes = held([P, PASSES * 2 * H], U8, "wa_codes")
         wa_sc = held([P, PASSES * H], U8, "wa_sc")
         for dst, src in ((wa_codes, wa_raw), (wa_sc, wa_sc_raw)):
-            for a in range(PASSES):
-                nc.gpsimd.tensor_copy(
-                    dst[:].bitcast(I32).rearrange("p (a t b e) -> p a t b e", a=PASSES, t=PACK, b=16)[:, a],
-                    src[:].bitcast(I32).rearrange("p (a b t e) -> p a t b e", a=PASSES, t=PACK, b=16)[:, a],
-                )
+            nc.vector.tensor_copy(
+                dst[:].bitcast(I32).rearrange("p (a t b e) -> p a t b e", a=PASSES, t=PACK, b=16),
+                src[:].bitcast(I32).rearrange("p (a b t e) -> p a t b e", a=PASSES, t=PACK, b=16),
+            )
 
         up_sc = held([P, S], U8, "up_sc")
         gw_sc = held([P, S], U8, "gw_sc")
@@ -245,7 +245,7 @@ def tile_list_gateway_rate_scores_kernel(
 
         def product(i, h):
             u, c0 = divmod(i * P, WC_COLS)
-            q_bank = bank("q%d_%d" % (i, h), "q")
+            q_bank = bank("q%d_%d" % (i, h), "back" if (i, h) == (0, 0) else "up")
             nc.tensor.matmul_mx(
                 q_bank[:],
                 lhsT=wc_codes[u][:, c0 : c0 + P].bitcast(E4M3),
@@ -260,12 +260,11 @@ def tile_list_gateway_rate_scores_kernel(
                 nc.vector.tensor_tensor(q_sb[i, h][:], q_bank[:], interf_sb[i][:, 0:HALF], ADD)
                 turned[i, h] = ring.tile([P, HALF], F32, name="turned")
                 nc.scalar.activation(turned[i, h][:], q_sb[i, h][:], TANH)
-                place(i, h, turned[i, h])
             else:
                 nc.scalar.copy(q_sb[i, h][:], q_bank[:])
 
         def shift_and_tanh(i, h):
-            sum_bank = bank("sum%d_%d" % (i, h), "sum")
+            sum_bank = bank("sum%d_%d" % (i, h), "gw")
             for c in range(CHUNKS):
                 cols = slice(c * P, (c + 1) * P)
                 j0 = h * HALF + c * P
@@ -297,24 +296,23 @@ def tile_list_gateway_rate_scores_kernel(
                 )
             else:
                 if h == 0:
-                    y_sb[i] = ring.tile([P, S], F32, name="y")
+                    y_sb[i] = held([P, S], F32, "y%d" % i)
                 nc.scalar.activation(y_sb[i][:, half], rates[:], COPY, scale=gain)
                 if h == HALVES - 1:
                     nc.vector.tensor_tensor(page[:].indirect(list_out[:]), y_sb[i][:], wgo_sb, MULT)
             if h == HALVES - 1:
                 nc.sync.dma_start(out[P * i : P * (i + 1), :], page[:])
 
-        units = [(i, h) for h in range(HALVES) for i in range(SPLIT_TILES)]
-        units = units + [(i, h) for i in range(SPLIT_TILES, ROW_TILES) for h in range(HALVES)]
         first_stage(0)
-        product(*units[0])
+        product(0, 0)
         first_stage(1)
-        for step in range(1, len(units) + 2):
-            if step < len(units):
-                product(*units[step])
-            if 2 <= step <= len(units):
-                shift_and_tanh(*units[step - 1])
-            if step >= 3:
-                turn_back(*units[step - 2])
-            if step in (2, 3):
-                quantise_wc(step - 1)
+        place(0, 0, turned[0, 0])
+        steps = [[(i, h)] for h in range(HALVES) for i in range(SPLIT_TILES)][1:]
+        steps = steps + [[(i, h) for h in range(HALVES)] for i in range(SPLIT_TILES, ROW_TILES)]
+        for n in range(len(steps) + 2):
+            if n in (1, 3):
+                quantise_wc(n // 2 + 1)
+            for lag, stage in enumerate((product, shift_and_tanh, turn_back)):
+                if 0 <= n - lag < len(steps):
+                    for unit in steps[n - lag]:
+                        stage(*unit)

from contextlib import ExitStack

import concourse.mybir as mybir
from concourse.masks import make_identity

K, H, N, T, S, T2 = 1024, 512, 768, 4096, 1024, 2048
FLOPS = 2 * (2 * K * H * S + H * N * S)

F32 = mybir.dt.float32
BF16 = mybir.dt.bfloat16
I32 = mybir.dt.int32
U32 = mybir.dt.uint32
U16 = mybir.dt.uint16
U8 = mybir.dt.uint8
E4M3 = mybir.dt.float8_e4m3fn_x4
E2M1 = mybir.dt.float4_e2m1fn_x4
MULT = mybir.AluOpType.mult
ADD = mybir.AluOpType.add
MAX = mybir.AluOpType.max
COPY = mybir.ActivationFunctionType.Copy
TANH = mybir.ActivationFunctionType.Tanh

P = 128
PACK = 4
PASSES = K // (P * PACK)
HALF = 512
HALVES = S // HALF
CHUNKS = HALF // P
ROW_TILES = N // P
WC_COLS = 256
PAGES = 3
SPLIT_TILES = 3
SHIFT_ROWS = 112
BANKS = {"up": 2, "gw": 3, "back": 3}


def tile_list_gateway_rate_scores_kernel(
    tc, tab_words, tab_scales, offs, offs2, offs3, wa_words, wa_scales, ga, wb, wc, interf, gr, wgo, out
):
    nc = tc.nc
    with ExitStack() as ctx:
        keep = ctx.enter_context(tc.tile_pool(name="keep", bufs=1))
        ring = ctx.enter_context(tc.tile_pool(name="ring", bufs=4))
        psum = ctx.enter_context(tc.psum_pool(name="psum", bufs=2))

        def held(shape, dtype, name, tag=None):
            return keep.tile(shape, dtype, name=name, tag=tag or name, align_bytes=64)

        def bank(name, tag):
            return psum.tile([P, HALF], F32, name=name, tag=tag, bufs=BANKS[tag])

        tab_sc = held([P, T], U8, "tab_sc")
        nc.vector.memset(tab_sc[:].bitcast(I32), 0)
        pages = [held([P, T2], F32, "page%d" % g) for g in range(PAGES)]
        for page in pages:
            nc.vector.memset(page[:], 0.0)

        gains_rows = held([P, P], F32, "gains_rows")
        nc.gpsimd.memset(gains_rows[:], 0.0)
        wa_sc_raw = held([P, PASSES * H], U8, "wa_sc_raw")
        nc.gpsimd.memset(wa_sc_raw[:].bitcast(I32), 0)
        up_sc_shifted = held([P, S], U8, "up_sc_shifted")
        nc.gpsimd.memset(up_sc_shifted[:].bitcast(I32), 0)
        ident = held([P, P], F32, "ident")
        make_identity(nc, ident[:])

        def load_list(name, src):
            tile = keep.tile([P, S // 16], U16, name=name)
            nc.sync.dma_start(tile[:], src)
            return tile

        list_up = load_list("list_up", offs)
        list_gw = load_list("list_gw", offs2)
        list_out = load_list("list_out", offs3)
        tab = [held([P, T], U32, "tab%d" % a) for a in range(PASSES)]
        wb_raw = [held([P, PACK, H], F32, "wb_raw%d" % a) for a in range(PASSES)]
        wa_raw = held([P, PASSES * 2 * H], U8, "wa_raw")

        def load_table(a, pieces):
            words = tab_words[a].rearrange("p t i -> p (t i)").bitcast(I32)
            for u in range(pieces):
                cols = slice(u * T // pieces, (u + 1) * T // pieces)
                nc.sync.dma_start(tab[a][:].bitcast(I32)[:, cols], words[:, cols])

        load_table(0, 4)
        nc.sync.dma_start(
            wa_raw[:].bitcast(I32).rearrange("p (a w) -> p a w", a=PASSES),
            wa_words.bitcast(I32).rearrange("a p w -> p a w"),
        )
        for a in range(PASSES):
            for q in range(4):
                nc.sync.dma_start(
                    tab_sc[32 * q + 4 * a : 32 * q + 4 * a + 4, :].bitcast(I32),
                    tab_scales[a, 4 * q : 4 * q + 4, :].bitcast(I32),
                )
        for a in range(PASSES):
            nc.sync.dma_start(
                wb_raw[a][:], wb[512 * a : 512 * (a + 1), :].rearrange("(p j) c -> p j c", j=PACK)
            )
        for q in range(4):
            nc.sync.dma_start(
                wa_sc_raw[32 * q : 32 * q + 4, :].bitcast(I32).rearrange("r (a w) -> r a w", a=PASSES),
                wa_scales[:, 4 * q : 4 * q + 4, :].bitcast(I32).rearrange("a r w -> r a w"),
            )
        nc.sync.dma_start(
            gains_rows[0:PACK, :].rearrange("t (b e) -> t b e", e=8),
            ga.rearrange("(b t e) -> t b e", t=PACK, e=8),
        )
        nc.sync.dma_start(gains_rows[PACK : PACK + ROW_TILES, :], gr.rearrange("(i p) -> i p", p=P))
        load_table(1, 1)

        gains_bank = bank("gains_bank", "back")
        nc.tensor.transpose(gains_bank[:, 0:P], gains_rows[:], ident[:])
        gains = held([P, 16], F32, "gains")
        nc.scalar.copy(gains[:], gains_bank[:, 0:16])

        wa_codes = held([P, PASSES * 2 * H], U8, "wa_codes")
        wa_sc = held([P, PASSES * H], U8, "wa_sc")
        for dst, src in ((wa_codes, wa_raw), (wa_sc, wa_sc_raw)):
            nc.vector.tensor_copy(
                dst[:].bitcast(I32).rearrange("p (a t b e) -> p a t b e", a=PASSES, t=PACK, b=16),
                src[:].bitcast(I32).rearrange("p (a b t e) -> p a t b e", a=PASSES, t=PACK, b=16),
            )

        up_sc = held([P, S], U8, "up_sc")
        gw_sc = held([P, S], U8, "gw_sc")
        nc.vector.tensor_copy(up_sc[:], tab_sc[:].indirect(list_up[:]))
        nc.vector.tensor_copy(gw_sc[:], tab_sc[:].indirect(list_gw[:]))
        nc.sync.dma_start(
            up_sc_shifted[0:SHIFT_ROWS, :].bitcast(I32), up_sc[4 : 4 + SHIFT_ROWS, :].bitcast(I32)
        )
        up0 = held([P, S], U32, "up0")
        gw0 = held([P, S], U32, "gw0")
        nc.vector.tensor_copy(up0[:], tab[0][:].indirect(list_up[:]))
        nc.vector.tensor_copy(gw0[:], tab[0][:].indirect(list_gw[:]))

        wb_codes, wb_sc = {}, {}

        def quantise_wb(a, pair, copy):
            rounded = held([P, 2 * P * PACK], BF16, "wb_bf%d_%d" % (a, pair))
            for u in range(2):
                copy(
                    rounded[:].rearrange("p (u b h i j) -> p u b h j i", u=2, b=16, h=2, i=4)[:, u],
                    wb_raw[a][:].rearrange("p j (b t h i) -> p t b h j i", t=PACK, h=2, i=4)[:, 2 * pair + u],
                )
            codes = held([P, 2 * P], U32, "wb_codes%d_%d" % (a, pair))
            scales = held([P, 2 * P], U8, "wb_sc%d_%d" % (a, pair))
            nc.vector.quantize_mx(codes[:].bitcast(E4M3), scales[:], rounded[:])
            wb_codes[a, pair] = codes
            wb_sc[a, pair] = scales

        for a in range(PASSES):
            for pair in range(2):
                quantise_wb(a, pair, nc.scalar.copy)

        up1, gw1 = [], []
        for h in range(HALVES):
            cut = slice(h * HALF // 16, (h + 1) * HALF // 16)
            for name, picked, order in (("up1_%d", up1, list_up), ("gw1_%d", gw1, list_gw)):
                tile = held([P, HALF], U32, name % h)
                nc.vector.tensor_copy(tile[:], tab[1][:].indirect(order[:, cut]))
                picked.append(tile)

        wc_raw = held([P, PACK, N], F32, "wc_raw", tag="wb_raw0")
        wc_by_slot = wc.rearrange("(b t e) n -> t b e n", t=PACK, e=8)
        for t in range(PACK):
            nc.sync.dma_start(wc_raw[:, t, :], wc_by_slot[t])
        first = held([P, 2, S], F32, "first", tag="wb_raw1")
        rest = held([P, ROW_TILES - 1, S], F32, "rest", tag="tab0")
        wgo_sb = first[:, 1, :]
        interf_sb = [first[:, 0, :]] + [rest[:, i, :] for i in range(ROW_TILES - 1)]
        for i in range(ROW_TILES):
            nc.sync.dma_start(interf_sb[i], interf[P * i : P * (i + 1), :])
            if i == 0:
                nc.sync.dma_start(wgo_sb, wgo)

        def up_pass(acc, h, t, a):
            cols = slice(h * HALF, (h + 1) * HALF)
            nc.tensor.matmul_mx(
                acc[:],
                lhsT=wa_codes[:, 2 * (a * H + t * P) : 2 * (a * H + (t + 1) * P)].bitcast(E2M1),
                lhsT_scale=wa_sc[:, a * H + t * P : a * H + (t + 1) * P],
                rhs=(up0[:, cols] if a == 0 else up1[h][:]).bitcast(E4M3),
                rhs_scale=(up_sc if a == 0 else up_sc_shifted)[:, cols],
                start=(a == 0),
                stop=(a == PASSES - 1),
            )

        def gw_pass(acc, h, c, t, a):
            j0 = h * HALF + c * P
            nc.tensor.matmul_mx(
                acc[:, t * P : (t + 1) * P],
                lhsT=wb_codes[a, t // 2][:, t % 2 * P : (t % 2 + 1) * P].bitcast(E4M3),
                lhsT_scale=wb_sc[a, t // 2][:, t % 2 * P : (t % 2 + 1) * P],
                rhs=(gw0[:, j0 : j0 + P] if a == 0 else gw1[h][:, c * P : (c + 1) * P]).bitcast(E4M3),
                rhs_scale=gw_sc[4 * a : P, j0 : j0 + P],
                start=(a == 0 and t == 0),
                stop=(a == PASSES - 1 and t == PACK - 1),
            )

        z_codes, z_sc = [], []

        def first_stage(h):
            scaled = held([P, PACK, HALF], F32, "scaled%d" % h)
            z_bf = held([P, HALF * PACK], BF16, "z_bf%d" % h)
            for t in range(PACK):
                up_bank = bank("up%d_%d" % (h, t), "up")
                for a in range(PASSES):
                    up_pass(up_bank, h, t, a)
                nc.scalar.activation(scaled[:, t, :], up_bank[:], COPY, scale=gains[:, t : t + 1])
            if h == 0:
                quantise_wc(0)
            for c in range(CHUNKS):
                gw_bank = bank("gw%d_%d" % (h, c), "gw")
                for a in range(PASSES):
                    for t in range(PACK):
                        gw_pass(gw_bank, h, c, t, a)
                nc.vector.tensor_tensor(
                    z_bf[:, c * HALF : (c + 1) * HALF].rearrange("p (g i t) -> p g t i", i=4, t=PACK),
                    gw_bank[:].rearrange("p (t g i) -> p g t i", t=PACK, i=4),
                    scaled[:, :, c * P : (c + 1) * P].rearrange("p t (g i) -> p g t i", i=4),
                    MAX,
                )
            codes = held([P, HALF], U32, "z_codes%d" % h)
            scales = held([P, HALF], U8, "z_sc%d" % h)
            nc.vector.quantize_mx(codes[:].bitcast(E4M3), scales[:], z_bf[:])
            z_codes.append(codes)
            z_sc.append(scales)

        wc_codes, wc_sc = [], []

        def quantise_wc(u):
            rounded = held([P, WC_COLS * PACK], BF16, "wc_bf%d" % u)
            nc.scalar.copy(
                rounded[:].rearrange("p (g i t) -> p g t i", i=4, t=PACK),
                wc_raw[:, :, u * WC_COLS : (u + 1) * WC_COLS].rearrange("p t (g i) -> p g t i", i=4),
            )
            codes = held([P, WC_COLS], U32, "wc_codes%d" % u)
            scales = held([P, WC_COLS], U8, "wc_sc%d" % u)
            nc.vector.quantize_mx(codes[:].bitcast(E4M3), scales[:], rounded[:])
            wc_codes.append(codes)
            wc_sc.append(scales)

        q_sb, turned, y_sb = {}, {}, {}

        def product(i, h):
            u, c0 = divmod(i * P, WC_COLS)
            q_bank = bank("q%d_%d" % (i, h), "back" if (i, h) == (0, 0) else "up")
            nc.tensor.matmul_mx(
                q_bank[:],
                lhsT=wc_codes[u][:, c0 : c0 + P].bitcast(E4M3),
                lhsT_scale=wc_sc[u][:, c0 : c0 + P],
                rhs=z_codes[h][:].bitcast(E4M3),
                rhs_scale=z_sc[h][:],
                start=True,
                stop=True,
            )
            q_sb[i, h] = ring.tile([P, HALF], F32, name="q_sb")
            if (i, h) == (0, 0):
                nc.vector.tensor_tensor(q_sb[i, h][:], q_bank[:], interf_sb[i][:, 0:HALF], ADD)
                turned[i, h] = ring.tile([P, HALF], F32, name="turned")
                nc.scalar.activation(turned[i, h][:], q_sb[i, h][:], TANH)
            else:
                nc.scalar.copy(q_sb[i, h][:], q_bank[:])

        def shift_and_tanh(i, h):
            sum_bank = bank("sum%d_%d" % (i, h), "gw")
            for c in range(CHUNKS):
                cols = slice(c * P, (c + 1) * P)
                j0 = h * HALF + c * P
                nc.tensor.matmul(
                    sum_bank[:, cols], q_sb[i, h][:, cols], ident[:], start=True, stop=False, is_transpose=True
                )
                nc.tensor.matmul(
                    sum_bank[:, cols], interf_sb[i][:, j0 : j0 + P], ident[:], start=False, stop=True, is_transpose=True
                )
            turned[i, h] = ring.tile([P, HALF], F32, name="turned")
            nc.scalar.activation(turned[i, h][:], sum_bank[:], TANH)

        def turn_back(i, h):
            back_bank = bank("back%d_%d" % (i, h), "back")
            for c in range(CHUNKS):
                cols = slice(c * P, (c + 1) * P)
                nc.tensor.transpose(back_bank[:, cols], turned[i, h][:, cols], ident[:])
            place(i, h, back_bank)

        def place(i, h, rates):
            half = slice(h * HALF, (h + 1) * HALF)
            page = pages[i % PAGES]
            gain = gains[:, PACK + i : PACK + i + 1]
            if i < SPLIT_TILES:
                y_half = held([P, HALF], F32, "y_half%d_%d" % (i, h))
                nc.scalar.activation(y_half[:], rates[:], COPY, scale=gain)
                nc.vector.tensor_tensor(
                    page[:].indirect(list_out[:, h * HALF // 16 : (h + 1) * HALF // 16]), y_half[:], wgo_sb[:, half], MULT
                )
            else:
                if h == 0:
                    y_sb[i] = held([P, S], F32, "y%d" % i)
                nc.scalar.activation(y_sb[i][:, half], rates[:], COPY, scale=gain)
                if h == HALVES - 1:
                    nc.vector.tensor_tensor(page[:].indirect(list_out[:]), y_sb[i][:], wgo_sb, MULT)
            if h == HALVES - 1:
                nc.sync.dma_start(out[P * i : P * (i + 1), :], page[:])

        first_stage(0)
        product(0, 0)
        first_stage(1)
        place(0, 0, turned[0, 0])
        steps = [[(i, h)] for h in range(HALVES) for i in range(SPLIT_TILES)][1:]
        steps = steps + [[(i, h) for h in range(HALVES)] for i in range(SPLIT_TILES, ROW_TILES)]
        for n in range(len(steps) + 2):
            if n in (1, 3):
                quantise_wc(n // 2 + 1)
            for lag, stage in enumerate((product, shift_and_tanh, turn_back)):
                if 0 <= n - lag < len(steps):
                    for unit in steps[n - lag]:
                        stage(*unit)
